import numpy as np
import ml_dtypes


def mxq(x, axis, fmt="e4m3"):
    dtype, down = {"e4m3": (ml_dtypes.float8_e4m3fn, 7), "e5m2": (ml_dtypes.float8_e5m2, 14)}[fmt]
    v = np.moveaxis(np.asarray(x, np.float32).astype(ml_dtypes.bfloat16).astype(np.float64), axis, -1)
    blocks = v.reshape(v.shape[:-1] + (-1, 32))
    amax = np.abs(blocks).max(-1, keepdims=True)
    byte = np.maximum(np.where(amax > 0, np.frexp(amax)[1] - 1 + 127, 0) - down, 1)
    scale = np.exp2(byte - 127.0)
    codes = (blocks / scale).astype(np.float32).astype(dtype).astype(np.float64)
    return np.moveaxis((codes * scale).reshape(v.shape), -1, axis)


WIDE = False


def mx_kscale(k):
    if not WIDE:
        return np.ones(k)
    levels = np.array([10, -10, 5, -5, 0])
    if k % 512:
        return np.exp2(np.random.permutation(np.resize(levels, k // 32))).repeat(32)
    a = np.empty((k // 512, 16))
    for p in range(k // 512):
        a[p, :8] = np.random.permutation(np.resize(levels, 8))
        for g in range(8):
            far = levels[np.abs(levels - a[p, g]) >= 10]
            a[p, g + 8] = far[np.random.randint(len(far))]
    return np.exp2(a.ravel()).repeat(32)


def f64(x):
    return np.asarray(x).astype(np.float64)


def striped(idx):
    return np.tile(np.asarray(idx).reshape(-1, 16).T, (8, 1)).astype(np.uint16)


def unstriped(offs):
    return offs[:16].T.reshape(-1).astype(np.int64)


E2M1 = np.array([0.0, 0.5, 1.0, 1.5, 2.0, 3.0, 4.0, 6.0, -0.0, -0.5, -1.0, -1.5, -2.0, -3.0, -4.0, -6.0])


def pack_weight(w, fmt):
    k, n = w.shape
    w = f64(np.asarray(w, np.float32).astype(ml_dtypes.bfloat16)).reshape(k // 32, 32, n)
    amax = np.abs(w).max(1)
    if fmt == "e4m3":
        byte = np.frexp(amax)[1] - 1 + 127 - 7
    else:
        mant, ex = np.frexp(amax / 6.0)
        byte = np.where(mant > 0.5, ex, ex - 1) + 127
    byte = np.clip(np.where(amax > 0, byte, 1), 1, 254)
    scaled = (w * np.exp2(127.0 - byte)[:, None, :]).reshape(k, n).astype(np.float32)
    by_word = np.ascontiguousarray(scaled.reshape(k // 512, 128, 4, n).transpose(0, 1, 3, 2))
    if fmt == "e4m3":
        words = by_word.astype(ml_dtypes.float8_e4m3fn).view(np.uint8)
    else:
        c = by_word.astype(ml_dtypes.float4_e2m1fn).view(np.uint8) & 0xF
        words = (c[..., 0::2] | (c[..., 1::2] << 4)).reshape(k // 512, 128, 2 * n)
    return np.ascontiguousarray(words), np.ascontiguousarray(byte.astype(np.uint8).reshape(k // 512, 16, n))


def unpack_weight(words, scales, fmt):
    g, _, n = scales.shape
    words = np.ascontiguousarray(words).reshape(g, 128, n, -1)
    if fmt == "e4m3":
        vals = words.view(ml_dtypes.float8_e4m3fn).astype(np.float64)
    else:
        nib = np.empty((g, 128, n, 4), np.uint8)
        nib[..., 0::2] = words & 0xF
        nib[..., 1::2] = words >> 4
        vals = E2M1[nib]
    vals = vals * np.repeat(np.exp2(scales.astype(np.float64) - 127.0), 8, axis=1)[..., None]
    return vals.transpose(0, 1, 3, 2).reshape(g * 512, n)


K, T, J, N = 1024, 2048, 512, 512


def setup_inputs():
    n = np.random.standard_normal
    idx = np.random.permutation(T)[:J]
    idx2 = np.random.permutation(T)[:J]
    fk = mx_kscale(K)
    xtp = pack_weight(n((K, T)) / fk[:, None], "e4m3")
    return {
        "xt_words": xtp[0],
        "xt_scales": xtp[1],
        "w": (n((K, N)) * 1 / np.sqrt(K) * fk[:, None]).astype(np.float32),
        "mg": (np.random.uniform(0.2, 1.0, (1, J))).astype(np.float32),
        "offs": striped(idx),
        "offs2": striped(idx2),
    }


def reference(xt_words, xt_scales, w, mg, offs, offs2):
    idx = unstriped(offs)
    idx2 = unstriped(offs2)
    xtu = unpack_weight(xt_words, xt_scales, "e4m3")
    wq = mxq(f64(w), 0, "e4m3")
    xtidxg = xtu[:, idx]
    p = wq.T @ xtidxg
    xtidx2g = xtu[:, idx2]
    q = wq.T @ xtidx2g
    y = np.square(np.maximum(f64(mg) - p + q, 0.0))
    return y

@@ -1,0 +1,182 @@
+from contextlib import ExitStack
+
+import concourse.mybir as mybir
+from concourse.masks import make_identity
+
+K, T, J, N = 1024, 2048, 512, 512
+FLOPS = 2 * 2 * K * J * N
+
+F32 = mybir.dt.float32
+BF16 = mybir.dt.bfloat16
+I32 = mybir.dt.int32
+U32 = mybir.dt.uint32
+U16 = mybir.dt.uint16
+U8 = mybir.dt.uint8
+FP8X4 = mybir.dt.float8_e4m3fn_x4
+ACT = mybir.ActivationFunctionType
+ALU = mybir.AluOpType
+
+P = 128
+PACK = 4
+K_PASS = P * PACK
+PASSES = K // K_PASS
+HALF = 256
+LIST_COLS = J // 16
+SCALAR_COLS = 192
+
+
+def tile_list_ranking_pairs_kernel(tc, xt_words, xt_scales, w, mg, offs, offs2, out):
+    nc = tc.nc
+    with ExitStack() as ctx:
+        keep = ctx.enter_context(tc.tile_pool(name="keep", bufs=1))
+        psum = ctx.enter_context(tc.psum_pool(name="psum", bufs=1))
+
+        list_p = keep.tile([P, LIST_COLS], U16, name="list_p")
+        list_q = keep.tile([P, LIST_COLS], U16, name="list_q")
+        words = [keep.tile([P, T], I32, name=f"words{z}", align_bytes=64) for z in range(PASSES)]
+        w_rows = [keep.tile([P, PACK, N], F32, name=f"w_rows{z}", align_bytes=64) for z in range(PASSES)]
+        scales = keep.tile([P, T], U8, name="scales", tag="scales_then_codes", align_bytes=64)
+        margin = keep.tile([P, J // P], F32, name="margin")
+        ident = keep.tile([P, P], F32, name="ident", align_bytes=64)
+
+        def load_words(z):
+            nc.sync.dma_start(words[z][:], xt_words[z].rearrange("p t r -> p (t r)").bitcast(I32))
+
+        def load_w(z):
+            rows = w[z * K_PASS : (z + 1) * K_PASS, :]
+            nc.sync.dma_start(w_rows[z][:], rows.rearrange("(p r) n -> p r n", r=PACK))
+
+        nc.gpsimd.memset(scales[:].bitcast(I32), 0)
+        nc.sync.dma_start(list_p[:], offs)
+        load_words(0)
+        nc.sync.dma_start(list_q[:], offs2)
+        load_w(0)
+        load_w(1)
+        load_words(1)
+        with nc.allow_non_contiguous_dma(reason="one margin to a partition and tile of slots"):
+            nc.sync.dma_start(margin[:], mg.rearrange("o (c p) -> p (o c)", p=P))
+        for quad in range(4):
+            nc.gpsimd.dma_start(
+                scales[32 * quad : 32 * quad + 4 * PASSES, :].bitcast(I32),
+                xt_scales[:, 4 * quad : 4 * quad + 4, :].bitcast(I32),
+            )
+        nc.vector.memset(ident[:], 0.0)
+        make_identity(nc, ident[:], nomemset=True)
+
+        def gather_words(picked, z, lst, cols):
+            nc.vector.tensor_copy(picked, words[z][:].bitcast(U32).indirect(lst[:, cols]))
+
+        def gather_scales(lst, name):
+            picked = keep.tile([P, J], U8, name=name, align_bytes=64)
+            nc.vector.tensor_copy(picked[:], scales[:].indirect(lst[:]))
+            return picked
+
+        def interleave(engine, grouped, z, cols):
+            dst = grouped[:, cols, :].rearrange("p (c i) r -> p c r i", i=4)
+            src = w_rows[z][:, :, cols].rearrange("p r (c i) -> p c r i", i=4)
+            if engine == "scalar":
+                nc.scalar.activation(dst, src, ACT.Copy)
+            else:
+                nc.vector.tensor_copy(dst, src)
+
+        def quantize(grouped, codes, plane, cols):
+            nc.vector.quantize_mx(
+                out=codes[:, cols].bitcast(FP8X4),
+                scales=plane[:, cols],
+                in_=grouped[:, cols, :].rearrange("p n r -> p (n r)"),
+            )
+
+        whole = slice(0, LIST_COLS)
+        first, second = slice(0, LIST_COLS // 2), slice(LIST_COLS // 2, LIST_COLS)
+
+        xp0 = keep.tile([P, J], U32, name="xp0", align_bytes=64)
+        xq0 = keep.tile([P, J], U32, name="xq0", align_bytes=64)
+        gather_words(xp0[:], 0, list_p, whole)
+        gather_words(xq0[:], 0, list_q, whole)
+        sp = gather_scales(list_p, "sp")
+        sq = gather_scales(list_q, "sq")
+
+        w_codes = keep.tile([P, PASSES * N], U32, name="w_codes", tag="scales_then_codes", align_bytes=64)
+        w_planes = [keep.tile([P, N], U8, name=f"w_plane{z}", align_bytes=64) for z in range(PASSES)]
+        wq0 = (w_codes[:, 0:N], w_planes[0])
+        wq1 = (w_codes[:, N : 2 * N], w_planes[1])
+
+        grouped0 = keep.tile([P, N, PACK], BF16, name="grouped0", tag="stage", align_bytes=64)
+        for cols in (slice(0, HALF), slice(HALF, N)):
+            interleave("scalar", grouped0, 0, cols)
+            quantize(grouped0, wq0[0], wq0[1], cols)
+
+        p_bank = [psum.tile([P, N], F32, name=f"p_bank{jt}", tag=f"bank{jt}") for jt in range(4)]
+        q_bank = [
+            [psum.tile([P, 2, HALF], F32, name=f"q_bank{jh}{nh}") for nh in range(2)] for jh in range(2)
+        ]
+
+        def mx(dst, tokens, local_jt, token_scales, jt, z, wq, cols, start, stop):
+            nc.tensor.matmul_mx(
+                out=dst,
+                lhsT=tokens[:, local_jt * P : (local_jt + 1) * P].bitcast(FP8X4),
+                lhsT_scale=token_scales[4 * z :, jt * P : (jt + 1) * P],
+                rhs=wq[0][:, cols].bitcast(FP8X4),
+                rhs_scale=wq[1][:, cols],
+                start=start,
+                stop=stop,
+            )
+
+        def n_half(nh):
+            return slice(nh * HALF, (nh + 1) * HALF)
+
+        for nh in range(2):
+            for jt in range(4):
+                mx(p_bank[jt][:, n_half(nh)], xp0, jt, sp, jt, 0, wq0, n_half(nh), nh == 0, False)
+        for jt in range(4):
+            for nh in range(2):
+                mx(q_bank[jt // 2][nh][:, jt % 2, :], xq0, jt, sq, jt, 0, wq0, n_half(nh), jt % 2 == 0, False)
+
+        grouped1 = keep.tile([P, N, PACK], BF16, name="grouped1", tag="stage", align_bytes=64)
+        interleave("scalar", grouped1, 1, slice(0, SCALAR_COLS))
+        interleave("vector", grouped1, 1, slice(SCALAR_COLS, N))
+        quantize(grouped1, wq1[0], wq1[1], slice(0, N))
+
+        x1 = keep.tile([P, 2 * J], U32, name="x1", tag="stage", align_bytes=64)
+        xp1 = [x1[:, jh * HALF : (jh + 1) * HALF] for jh in range(2)]
+        xq1 = [x1[:, J + jh * HALF : J + (jh + 1) * HALF] for jh in range(2)]
+        for picked, lst in ((xp1, list_p), (xq1, list_q)):
+            for jh, cols in enumerate((first, second)):
+                gather_words(picked[jh], 1, lst, cols)
+
+        for jt in range(4):
+            mx(p_bank[jt][:], xp1[jt // 2], jt % 2, sp, jt, 1, wq1, slice(0, N), False, True)
+        for jh in range(2):
+            for nh in range(2):
+                for a in range(2):
+                    mx(q_bank[jh][nh][:, a, :], xq1[jh], a, sq, 2 * jh + a, 1, wq1, n_half(nh), False, a == 1)
+
+        slack = [keep.tile([P, 2, N], F32, name=f"slack{jh}", align_bytes=64) for jh in range(2)]
+        for jt in range(4):
+            nc.scalar.activation(
+                slack[jt // 2][:, jt % 2, :], p_bank[jt][:], ACT.Identity, bias=margin[:, jt : jt + 1], scale=-1.0
+            )
+
+        for jh in range(2):
+            for nh in range(2):
+                raised = keep.tile([P, 2, HALF], F32, name=f"raised{jh}{nh}", align_bytes=64)
+                nc.vector.scalar_tensor_tensor(
+                    raised[:], slack[jh][:, :, n_half(nh)], -1.0, q_bank[jh][nh][:], ALU.mult, ALU.max
+                )
+                hinge = psum.tile([P, 2, HALF], F32, name=f"hinge{jh}{nh}", tag=f"bank{2 * jh + nh}")
+                blocks = [(a, b) for b in range(2) for a in range(2)]
+                for i, (a, b) in enumerate(blocks):
+                    n0 = nh * HALF + b * P
+                    nc.tensor.matmul(
+                        hinge[:, b, a * P : (a + 1) * P], slack[jh][:, a, n0 : n0 + P], ident[:],
+                        start=(i == 0), stop=False, is_transpose=True,
+                    )
+                for i, (a, b) in enumerate(blocks):
+                    nc.tensor.matmul(
+                        hinge[:, b, a * P : (a + 1) * P], raised[:, a, b * P : (b + 1) * P], ident[:],
+                        start=False, stop=(i == len(blocks) - 1), is_transpose=True,
+                    )
+                result = keep.tile([P, 2, HALF], F32, name=f"result{jh}{nh}", align_bytes=64)
+                nc.scalar.activation(result[:], hinge[:], ACT.Square)
+                rows = out[n_half(nh), jh * HALF : (jh + 1) * HALF]
+                nc.sync.dma_start(rows.rearrange("(b p) j -> p b j", p=P), result[:])

@@ -33,9 +33,11 @@ def tile_list_ranking_pairs_kernel(tc, xt_words, xt_scales, w, mg, offs, offs2, 
 
         list_p = keep.tile([P, LIST_COLS], U16, name="list_p")
         list_q = keep.tile([P, LIST_COLS], U16, name="list_q")
-        words = [keep.tile([P, T], I32, name=f"words{z}", align_bytes=64) for z in range(PASSES)]
+        words = [
+            keep.tile([P, T], I32, name=f"words{z}", tag=f"slot_words{z}", align_bytes=64) for z in range(PASSES)
+        ]
         w_rows = [keep.tile([P, PACK, N], F32, name=f"w_rows{z}", align_bytes=64) for z in range(PASSES)]
-        scales = keep.tile([P, T], U8, name="scales", tag="scales_then_codes", align_bytes=64)
+        scales = keep.tile([P, T], U8, name="scales", align_bytes=64)
         margin = keep.tile([P, J // P], F32, name="margin")
         ident = keep.tile([P, P], F32, name="ident", align_bytes=64)
 
@@ -48,18 +50,18 @@ def tile_list_ranking_pairs_kernel(tc, xt_words, xt_scales, w, mg, offs, offs2, 
 
         nc.gpsimd.memset(scales[:].bitcast(I32), 0)
         nc.sync.dma_start(list_p[:], offs)
-        load_words(0)
         nc.sync.dma_start(list_q[:], offs2)
+        for quad in range(4):
+            nc.sync.dma_start(
+                scales[32 * quad : 32 * quad + 4 * PASSES, :].bitcast(I32),
+                xt_scales[:, 4 * quad : 4 * quad + 4, :].bitcast(I32),
+            )
         load_w(0)
+        load_words(0)
         load_w(1)
         load_words(1)
         with nc.allow_non_contiguous_dma(reason="one margin to a partition and tile of slots"):
             nc.sync.dma_start(margin[:], mg.rearrange("o (c p) -> p (o c)", p=P))
-        for quad in range(4):
-            nc.gpsimd.dma_start(
-                scales[32 * quad : 32 * quad + 4 * PASSES, :].bitcast(I32),
-                xt_scales[:, 4 * quad : 4 * quad + 4, :].bitcast(I32),
-            )
         nc.vector.memset(ident[:], 0.0)
         make_identity(nc, ident[:], nomemset=True)
 
@@ -71,44 +73,39 @@ def tile_list_ranking_pairs_kernel(tc, xt_words, xt_scales, w, mg, offs, offs2, 
             nc.vector.tensor_copy(picked[:], scales[:].indirect(lst[:]))
             return picked
 
-        def interleave(engine, grouped, z, cols):
-            dst = grouped[:, cols, :].rearrange("p (c i) r -> p c r i", i=4)
-            src = w_rows[z][:, :, cols].rearrange("p r (c i) -> p c r i", i=4)
-            if engine == "scalar":
-                nc.scalar.activation(dst, src, ACT.Copy)
-            else:
-                nc.vector.tensor_copy(dst, src)
-
-        def quantize(grouped, codes, plane, cols):
+        def quantize_w(z, tag):
+            grouped = keep.tile([P, N, PACK], BF16, name=f"grouped{z}", tag=tag, align_bytes=64)
+            views = [
+                (
+                    grouped[:, cols, :].rearrange("p (c i) r -> p c r i", i=4),
+                    w_rows[z][:, :, cols].rearrange("p r (c i) -> p c r i", i=4),
+                )
+                for cols in (slice(0, SCALAR_COLS), slice(SCALAR_COLS, N))
+            ]
+            nc.scalar.activation(views[0][0], views[0][1], ACT.Copy)
+            nc.vector.tensor_copy(views[1][0], views[1][1])
+            codes = keep.tile([P, N], U32, name=f"w_codes{z}", align_bytes=64)
+            plane = keep.tile([P, N], U8, name=f"w_plane{z}", align_bytes=64)
             nc.vector.quantize_mx(
-                out=codes[:, cols].bitcast(FP8X4),
-                scales=plane[:, cols],
-                in_=grouped[:, cols, :].rearrange("p n r -> p (n r)"),
+                out=codes[:].bitcast(FP8X4), scales=plane[:], in_=grouped[:].rearrange("p n r -> p (n r)")
             )
+            return codes, plane
 
         whole = slice(0, LIST_COLS)
         first, second = slice(0, LIST_COLS // 2), slice(LIST_COLS // 2, LIST_COLS)
 
-        xp0 = keep.tile([P, J], U32, name="xp0", align_bytes=64)
-        xq0 = keep.tile([P, J], U32, name="xq0", align_bytes=64)
-        gather_words(xp0[:], 0, list_p, whole)
-        gather_words(xq0[:], 0, list_q, whole)
         sp = gather_scales(list_p, "sp")
         sq = gather_scales(list_q, "sq")
-
-        w_codes = keep.tile([P, PASSES * N], U32, name="w_codes", tag="scales_then_codes", align_bytes=64)
-        w_planes = [keep.tile([P, N], U8, name=f"w_plane{z}", align_bytes=64) for z in range(PASSES)]
-        wq0 = (w_codes[:, 0:N], w_planes[0])
-        wq1 = (w_codes[:, N : 2 * N], w_planes[1])
-
-        grouped0 = keep.tile([P, N, PACK], BF16, name="grouped0", tag="stage", align_bytes=64)
-        for cols in (slice(0, HALF), slice(HALF, N)):
-            interleave("scalar", grouped0, 0, cols)
-            quantize(grouped0, wq0[0], wq0[1], cols)
+        wq0 = quantize_w(0, "slot_stage")
+        x0 = keep.tile([P, 2 * J], U32, name="x0", tag="slot_stage", align_bytes=64)
+        xp0, xq0 = x0[:, 0:J], x0[:, J : 2 * J]
+        gather_words(xp0, 0, list_p, whole)
+        gather_words(xq0, 0, list_q, whole)
 
         p_bank = [psum.tile([P, N], F32, name=f"p_bank{jt}", tag=f"bank{jt}") for jt in range(4)]
         q_bank = [
-            [psum.tile([P, 2, HALF], F32, name=f"q_bank{jh}{nh}") for nh in range(2)] for jh in range(2)
+            [psum.tile([P, 2, HALF], F32, name=f"q_bank{jh}{nh}", tag=f"bank{4 + 2 * jh + nh}") for nh in range(2)]
+            for jh in range(2)
         ]
 
         def mx(dst, tokens, local_jt, token_scales, jt, z, wq, cols, start, stop):
@@ -125,19 +122,15 @@ def tile_list_ranking_pairs_kernel(tc, xt_words, xt_scales, w, mg, offs, offs2, 
         def n_half(nh):
             return slice(nh * HALF, (nh + 1) * HALF)
 
-        for nh in range(2):
-            for jt in range(4):
-                mx(p_bank[jt][:, n_half(nh)], xp0, jt, sp, jt, 0, wq0, n_half(nh), nh == 0, False)
+        for jt in range(4):
+            mx(p_bank[jt][:], xp0, jt, sp, jt, 0, wq0, slice(0, N), True, False)
         for jt in range(4):
             for nh in range(2):
                 mx(q_bank[jt // 2][nh][:, jt % 2, :], xq0, jt, sq, jt, 0, wq0, n_half(nh), jt % 2 == 0, False)
 
-        grouped1 = keep.tile([P, N, PACK], BF16, name="grouped1", tag="stage", align_bytes=64)
-        interleave("scalar", grouped1, 1, slice(0, SCALAR_COLS))
-        interleave("vector", grouped1, 1, slice(SCALAR_COLS, N))
-        quantize(grouped1, wq1[0], wq1[1], slice(0, N))
+        wq1 = quantize_w(1, "slot_words0")
 
-        x1 = keep.tile([P, 2 * J], U32, name="x1", tag="stage", align_bytes=64)
+        x1 = keep.tile([P, 2 * J], U32, name="x1", tag="slot_words0", align_bytes=64)
         xp1 = [x1[:, jh * HALF : (jh + 1) * HALF] for jh in range(2)]
         xq1 = [x1[:, J + jh * HALF : J + (jh + 1) * HALF] for jh in range(2)]
         for picked, lst in ((xp1, list_p), (xq1, list_q)):
@@ -157,26 +150,35 @@ def tile_list_ranking_pairs_kernel(tc, xt_words, xt_scales, w, mg, offs, offs2, 
                 slack[jt // 2][:, jt % 2, :], p_bank[jt][:], ACT.Identity, bias=margin[:, jt : jt + 1], scale=-1.0
             )
 
-        for jh in range(2):
-            for nh in range(2):
-                raised = keep.tile([P, 2, HALF], F32, name=f"raised{jh}{nh}", align_bytes=64)
-                nc.vector.scalar_tensor_tensor(
-                    raised[:], slack[jh][:, :, n_half(nh)], -1.0, q_bank[jh][nh][:], ALU.mult, ALU.max
+        def finish(jh, n_tiles, bank):
+            nh, b0, count = n_tiles[0] // 2, n_tiles[0] % 2, len(n_tiles)
+            n_cols = slice(n_tiles[0] * P, (n_tiles[-1] + 1) * P)
+            name = f"{jh}{n_tiles[0]}"
+            raised = keep.tile([P, 2, count * P], F32, name=f"raised{name}", align_bytes=64)
+            nc.vector.scalar_tensor_tensor(
+                raised[:], slack[jh][:, :, n_cols], -1.0, q_bank[jh][nh][:, :, b0 * P : (b0 + count) * P],
+                ALU.mult, ALU.max,
+            )
+            hinge = psum.tile([P, count, HALF], F32, name=f"hinge{name}", tag=f"bank{bank}")
+            blocks = [(a, b) for b in range(count) for a in range(2)]
+            for i, (a, b) in enumerate(blocks):
+                n0 = n_cols.start + b * P
+                nc.tensor.matmul(
+                    hinge[:, b, a * P : (a + 1) * P], slack[jh][:, a, n0 : n0 + P], ident[:],
+                    start=(i == 0), stop=False, is_transpose=True,
                 )
-                hinge = psum.tile([P, 2, HALF], F32, name=f"hinge{jh}{nh}", tag=f"bank{2 * jh + nh}")
-                blocks = [(a, b) for b in range(2) for a in range(2)]
-                for i, (a, b) in enumerate(blocks):
-                    n0 = nh * HALF + b * P
-                    nc.tensor.matmul(
-                        hinge[:, b, a * P : (a + 1) * P], slack[jh][:, a, n0 : n0 + P], ident[:],
-                        start=(i == 0), stop=False, is_transpose=True,
-                    )
-                for i, (a, b) in enumerate(blocks):
-                    nc.tensor.matmul(
-                        hinge[:, b, a * P : (a + 1) * P], raised[:, a, b * P : (b + 1) * P], ident[:],
-                        start=False, stop=(i == len(blocks) - 1), is_transpose=True,
-                    )
-                result = keep.tile([P, 2, HALF], F32, name=f"result{jh}{nh}", align_bytes=64)
-                nc.scalar.activation(result[:], hinge[:], ACT.Square)
-                rows = out[n_half(nh), jh * HALF : (jh + 1) * HALF]
-                nc.sync.dma_start(rows.rearrange("(b p) j -> p b j", p=P), result[:])
+            for i, (a, b) in enumerate(blocks):
+                nc.tensor.matmul(
+                    hinge[:, b, a * P : (a + 1) * P], raised[:, a, b * P : (b + 1) * P], ident[:],
+                    start=False, stop=(i == len(blocks) - 1), is_transpose=True,
+                )
+            result = keep.tile([P, count, HALF], F32, name=f"result{name}", align_bytes=64)
+            nc.scalar.activation(result[:], hinge[:], ACT.Square)
+            rows = out[n_cols, jh * HALF : (jh + 1) * HALF]
+            nc.sync.dma_start(rows.rearrange("(b p) j -> p b j", p=P), result[:])
+
+        finish(0, [0, 1], 0)
+        finish(0, [2, 3], 1)
+        finish(1, [0, 1], 2)
+        finish(1, [2], 3)
+        finish(1, [3], 4)

@@ -48,7 +48,9 @@ def tile_list_ranking_pairs_kernel(tc, xt_words, xt_scales, w, mg, offs, offs2, 
             rows = w[z * K_PASS : (z + 1) * K_PASS, :]
             nc.sync.dma_start(w_rows[z][:], rows.rearrange("(p r) n -> p r n", r=PACK))
 
+        margin_rows = keep.tile([P, P], F32, name="margin_rows", align_bytes=64)
         nc.gpsimd.memset(scales[:].bitcast(I32), 0)
+        nc.vector.memset(margin_rows[:], 0.0)
         nc.sync.dma_start(list_p[:], offs)
         nc.sync.dma_start(list_q[:], offs2)
         for quad in range(4):
@@ -56,14 +58,16 @@ def tile_list_ranking_pairs_kernel(tc, xt_words, xt_scales, w, mg, offs, offs2, 
                 scales[32 * quad : 32 * quad + 4 * PASSES, :].bitcast(I32),
                 xt_scales[:, 4 * quad : 4 * quad + 4, :].bitcast(I32),
             )
+        nc.sync.dma_start(margin_rows[0 : J // P, :], mg.rearrange("o (c p) -> (o c) p", p=P))
         load_w(0)
         load_words(0)
         load_w(1)
         load_words(1)
-        with nc.allow_non_contiguous_dma(reason="one margin to a partition and tile of slots"):
-            nc.sync.dma_start(margin[:], mg.rearrange("o (c p) -> p (o c)", p=P))
         nc.vector.memset(ident[:], 0.0)
         make_identity(nc, ident[:], nomemset=True)
+        margin_turned = psum.tile([P, P], F32, name="margin_turned", tag="bank7")
+        nc.tensor.transpose(margin_turned[:], margin_rows[:], ident[:])
+        nc.scalar.activation(margin[:], margin_turned[:, 0 : J // P], ACT.Copy)
 
         def gather_words(picked, z, lst, cols):
             nc.vector.tensor_copy(picked, words[z][:].bitcast(U32).indirect(lst[:, cols]))
@@ -146,11 +150,13 @@ def tile_list_ranking_pairs_kernel(tc, xt_words, xt_scales, w, mg, offs, offs2, 
 
         slack = [keep.tile([P, 2, N], F32, name=f"slack{jh}", align_bytes=64) for jh in range(2)]
         for jt in range(4):
+            cols = slice(0, N if jt < 3 else HALF)
             nc.scalar.activation(
-                slack[jt // 2][:, jt % 2, :], p_bank[jt][:], ACT.Identity, bias=margin[:, jt : jt + 1], scale=-1.0
+                slack[jt // 2][:, jt % 2, cols], p_bank[jt][:, cols], ACT.Identity,
+                bias=margin[:, jt : jt + 1], scale=-1.0,
             )
 
-        def finish(jh, n_tiles, bank):
+        def finish(jh, n_tiles, bank, queue=nc.sync):
             nh, b0, count = n_tiles[0] // 2, n_tiles[0] % 2, len(n_tiles)
             n_cols = slice(n_tiles[0] * P, (n_tiles[-1] + 1) * P)
             name = f"{jh}{n_tiles[0]}"
@@ -175,10 +181,13 @@ def tile_list_ranking_pairs_kernel(tc, xt_words, xt_scales, w, mg, offs, offs2, 
             result = keep.tile([P, count, HALF], F32, name=f"result{name}", align_bytes=64)
             nc.scalar.activation(result[:], hinge[:], ACT.Square)
             rows = out[n_cols, jh * HALF : (jh + 1) * HALF]
-            nc.sync.dma_start(rows.rearrange("(b p) j -> p b j", p=P), result[:])
+            queue.dma_start(rows.rearrange("(b p) j -> p b j", p=P), result[:])
 
         finish(0, [0, 1], 0)
         finish(0, [2, 3], 1)
+        nc.vector.tensor_scalar(
+            slack[1][:, 1, HALF:N], p_bank[3][:, HALF:N], -1.0, margin[:, 3:4], ALU.mult, ALU.add
+        )
         finish(1, [0, 1], 2)
         finish(1, [2], 3)
-        finish(1, [3], 4)
+        finish(1, [3], 4, nc.scalar)

from contextlib import ExitStack

import concourse.mybir as mybir
from concourse.masks import make_identity

K, T, J, N = 1024, 2048, 512, 512
FLOPS = 2 * 2 * K * J * N

F32 = mybir.dt.float32
BF16 = mybir.dt.bfloat16
I32 = mybir.dt.int32
U32 = mybir.dt.uint32
U16 = mybir.dt.uint16
U8 = mybir.dt.uint8
FP8X4 = mybir.dt.float8_e4m3fn_x4
ACT = mybir.ActivationFunctionType
ALU = mybir.AluOpType

P = 128
PACK = 4
K_PASS = P * PACK
PASSES = K // K_PASS
HALF = 256
LIST_COLS = J // 16
SCALAR_COLS = 192


def tile_list_ranking_pairs_kernel(tc, xt_words, xt_scales, w, mg, offs, offs2, out):
    nc = tc.nc
    with ExitStack() as ctx:
        keep = ctx.enter_context(tc.tile_pool(name="keep", bufs=1))
        psum = ctx.enter_context(tc.psum_pool(name="psum", bufs=1))

        list_p = keep.tile([P, LIST_COLS], U16, name="list_p")
        list_q = keep.tile([P, LIST_COLS], U16, name="list_q")
        words = [
            keep.tile([P, T], I32, name=f"words{z}", tag=f"slot_words{z}", align_bytes=64) for z in range(PASSES)
        ]
        w_rows = [keep.tile([P, PACK, N], F32, name=f"w_rows{z}", align_bytes=64) for z in range(PASSES)]
        scales = keep.tile([P, T], U8, name="scales", align_bytes=64)
        margin = keep.tile([P, J // P], F32, name="margin")
        ident = keep.tile([P, P], F32, name="ident", align_bytes=64)

        def load_words(z):
            nc.sync.dma_start(words[z][:], xt_words[z].rearrange("p t r -> p (t r)").bitcast(I32))

        def load_w(z):
            rows = w[z * K_PASS : (z + 1) * K_PASS, :]
            nc.sync.dma_start(w_rows[z][:], rows.rearrange("(p r) n -> p r n", r=PACK))

        margin_rows = keep.tile([P, P], F32, name="margin_rows", align_bytes=64)
        nc.gpsimd.memset(scales[:].bitcast(I32), 0)
        nc.vector.memset(margin_rows[:], 0.0)
        nc.sync.dma_start(list_p[:], offs)
        nc.sync.dma_start(list_q[:], offs2)
        for quad in range(4):
            nc.sync.dma_start(
                scales[32 * quad : 32 * quad + 4 * PASSES, :].bitcast(I32),
                xt_scales[:, 4 * quad : 4 * quad + 4, :].bitcast(I32),
            )
        nc.sync.dma_start(margin_rows[0 : J // P, :], mg.rearrange("o (c p) -> (o c) p", p=P))
        load_w(0)
        load_words(0)
        load_w(1)
        load_words(1)
        nc.vector.memset(ident[:], 0.0)
        make_identity(nc, ident[:], nomemset=True)
        margin_turned = psum.tile([P, P], F32, name="margin_turned", tag="bank7")
        nc.tensor.transpose(margin_turned[:], margin_rows[:], ident[:])
        nc.scalar.activation(margin[:], margin_turned[:, 0 : J // P], ACT.Copy)

        def gather_words(picked, z, lst, cols):
            nc.vector.tensor_copy(picked, words[z][:].bitcast(U32).indirect(lst[:, cols]))

        def gather_scales(lst, name):
            picked = keep.tile([P, J], U8, name=name, align_bytes=64)
            nc.vector.tensor_copy(picked[:], scales[:].indirect(lst[:]))
            return picked

        def quantize_w(z, tag):
            grouped = keep.tile([P, N, PACK], BF16, name=f"grouped{z}", tag=tag, align_bytes=64)
            views = [
                (
                    grouped[:, cols, :].rearrange("p (c i) r -> p c r i", i=4),
                    w_rows[z][:, :, cols].rearrange("p r (c i) -> p c r i", i=4),
                )
                for cols in (slice(0, SCALAR_COLS), slice(SCALAR_COLS, N))
            ]
            nc.scalar.activation(views[0][0], views[0][1], ACT.Copy)
            nc.vector.tensor_copy(views[1][0], views[1][1])
            codes = keep.tile([P, N], U32, name=f"w_codes{z}", align_bytes=64)
            plane = keep.tile([P, N], U8, name=f"w_plane{z}", align_bytes=64)
            nc.vector.quantize_mx(
                out=codes[:].bitcast(FP8X4), scales=plane[:], in_=grouped[:].rearrange("p n r -> p (n r)")
            )
            return codes, plane

        whole = slice(0, LIST_COLS)
        first, second = slice(0, LIST_COLS // 2), slice(LIST_COLS // 2, LIST_COLS)

        sp = gather_scales(list_p, "sp")
        sq = gather_scales(list_q, "sq")
        wq0 = quantize_w(0, "slot_stage")
        x0 = keep.tile([P, 2 * J], U32, name="x0", tag="slot_stage", align_bytes=64)
        xp0, xq0 = x0[:, 0:J], x0[:, J : 2 * J]
        gather_words(xp0, 0, list_p, whole)
        gather_words(xq0, 0, list_q, whole)

        p_bank = [psum.tile([P, N], F32, name=f"p_bank{jt}", tag=f"bank{jt}") for jt in range(4)]
        q_bank = [
            [psum.tile([P, 2, HALF], F32, name=f"q_bank{jh}{nh}", tag=f"bank{4 + 2 * jh + nh}") for nh in range(2)]
            for jh in range(2)
        ]

        def mx(dst, tokens, local_jt, token_scales, jt, z, wq, cols, start, stop):
            nc.tensor.matmul_mx(
                out=dst,
                lhsT=tokens[:, local_jt * P : (local_jt + 1) * P].bitcast(FP8X4),
                lhsT_scale=token_scales[4 * z :, jt * P : (jt + 1) * P],
                rhs=wq[0][:, cols].bitcast(FP8X4),
                rhs_scale=wq[1][:, cols],
                start=start,
                stop=stop,
            )

        def n_half(nh):
            return slice(nh * HALF, (nh + 1) * HALF)

        for jt in range(4):
            mx(p_bank[jt][:], xp0, jt, sp, jt, 0, wq0, slice(0, N), True, False)
        for jt in range(4):
            for nh in range(2):
                mx(q_bank[jt // 2][nh][:, jt % 2, :], xq0, jt, sq, jt, 0, wq0, n_half(nh), jt % 2 == 0, False)

        wq1 = quantize_w(1, "slot_words0")

        x1 = keep.tile([P, 2 * J], U32, name="x1", tag="slot_words0", align_bytes=64)
        xp1 = [x1[:, jh * HALF : (jh + 1) * HALF] for jh in range(2)]
        xq1 = [x1[:, J + jh * HALF : J + (jh + 1) * HALF] for jh in range(2)]
        for picked, lst in ((xp1, list_p), (xq1, list_q)):
            for jh, cols in enumerate((first, second)):
                gather_words(picked[jh], 1, lst, cols)

        for jt in range(4):
            mx(p_bank[jt][:], xp1[jt // 2], jt % 2, sp, jt, 1, wq1, slice(0, N), False, True)
        for jh in range(2):
            for nh in range(2):
                for a in range(2):
                    mx(q_bank[jh][nh][:, a, :], xq1[jh], a, sq, 2 * jh + a, 1, wq1, n_half(nh), False, a == 1)

        slack = [keep.tile([P, 2, N], F32, name=f"slack{jh}", align_bytes=64) for jh in range(2)]
        for jt in range(4):
            cols = slice(0, N if jt < 3 else HALF)
            nc.scalar.activation(
                slack[jt // 2][:, jt % 2, cols], p_bank[jt][:, cols], ACT.Identity,
                bias=margin[:, jt : jt + 1], scale=-1.0,
            )

        def finish(jh, n_tiles, bank, queue=nc.sync):
            nh, b0, count = n_tiles[0] // 2, n_tiles[0] % 2, len(n_tiles)
            n_cols = slice(n_tiles[0] * P, (n_tiles[-1] + 1) * P)
            name = f"{jh}{n_tiles[0]}"
            raised = keep.tile([P, 2, count * P], F32, name=f"raised{name}", align_bytes=64)
            nc.vector.scalar_tensor_tensor(
                raised[:], slack[jh][:, :, n_cols], -1.0, q_bank[jh][nh][:, :, b0 * P : (b0 + count) * P],
                ALU.mult, ALU.max,
            )
            hinge = psum.tile([P, count, HALF], F32, name=f"hinge{name}", tag=f"bank{bank}")
            blocks = [(a, b) for b in range(count) for a in range(2)]
            for i, (a, b) in enumerate(blocks):
                n0 = n_cols.start + b * P
                nc.tensor.matmul(
                    hinge[:, b, a * P : (a + 1) * P], slack[jh][:, a, n0 : n0 + P], ident[:],
                    start=(i == 0), stop=False, is_transpose=True,
                )
            for i, (a, b) in enumerate(blocks):
                nc.tensor.matmul(
                    hinge[:, b, a * P : (a + 1) * P], raised[:, a, b * P : (b + 1) * P], ident[:],
                    start=False, stop=(i == len(blocks) - 1), is_transpose=True,
                )
            result = keep.tile([P, count, HALF], F32, name=f"result{name}", align_bytes=64)
            nc.scalar.activation(result[:], hinge[:], ACT.Square)
            rows = out[n_cols, jh * HALF : (jh + 1) * HALF]
            queue.dma_start(rows.rearrange("(b p) j -> p b j", p=P), result[:])

        finish(0, [0, 1], 0)
        finish(0, [2, 3], 1)
        nc.vector.tensor_scalar(
            slack[1][:, 1, HALF:N], p_bank[3][:, HALF:N], -1.0, margin[:, 3:4], ALU.mult, ALU.add
        )
        finish(1, [0, 1], 2)
        finish(1, [2], 3)
        finish(1, [3], 4, nc.scalar)
